import numpy as np
import ml_dtypes


def mxq(x, axis, fmt="e4m3"):
    dtype, down = {"e4m3": (ml_dtypes.float8_e4m3fn, 7), "e5m2": (ml_dtypes.float8_e5m2, 14)}[fmt]
    v = np.moveaxis(np.asarray(x, np.float32).astype(ml_dtypes.bfloat16).astype(np.float64), axis, -1)
    blocks = v.reshape(v.shape[:-1] + (-1, 32))
    amax = np.abs(blocks).max(-1, keepdims=True)
    byte = np.maximum(np.where(amax > 0, np.frexp(amax)[1] - 1 + 127, 0) - down, 1)
    scale = np.exp2(byte - 127.0)
    codes = (blocks / scale).astype(np.float32).astype(dtype).astype(np.float64)
    return np.moveaxis((codes * scale).reshape(v.shape), -1, axis)


WIDE = False


def mx_kscale(k):
    if not WIDE:
        return np.ones(k)
    levels = np.array([10, -10, 5, -5, 0])
    if k % 512:
        return np.exp2(np.random.permutation(np.resize(levels, k // 32))).repeat(32)
    a = np.empty((k // 512, 16))
    for p in range(k // 512):
        a[p, :8] = np.random.permutation(np.resize(levels, 8))
        for g in range(8):
            far = levels[np.abs(levels - a[p, g]) >= 10]
            a[p, g + 8] = far[np.random.randint(len(far))]
    return np.exp2(a.ravel()).repeat(32)


def f64(x):
    return np.asarray(x).astype(np.float64)


def striped8(idx):
    return np.asarray(idx).reshape(8, -1, 16).transpose(0, 2, 1).reshape(128, -1).astype(np.uint16)


def unstriped8(offs):
    return offs.reshape(8, 16, -1).transpose(0, 2, 1).reshape(8, -1).astype(np.int64)


def pick8(x, idx, run):
    r = np.arange(len(x))
    return x[r[:, None], idx[r % (8 * run) // run]]


E2M1 = np.array([0.0, 0.5, 1.0, 1.5, 2.0, 3.0, 4.0, 6.0, -0.0, -0.5, -1.0, -1.5, -2.0, -3.0, -4.0, -6.0])


def pack_weight(w, fmt):
    k, n = w.shape
    w = f64(np.asarray(w, np.float32).astype(ml_dtypes.bfloat16)).reshape(k // 32, 32, n)
    amax = np.abs(w).max(1)
    if fmt == "e4m3":
        byte = np.frexp(amax)[1] - 1 + 127 - 7
    else:
        mant, ex = np.frexp(amax / 6.0)
        byte = np.where(mant > 0.5, ex, ex - 1) + 127
    byte = np.clip(np.where(amax > 0, byte, 1), 1, 254)
    scaled = (w * np.exp2(127.0 - byte)[:, None, :]).reshape(k, n).astype(np.float32)
    by_word = np.ascontiguousarray(scaled.reshape(k // 512, 128, 4, n).transpose(0, 1, 3, 2))
    if fmt == "e4m3":
        words = by_word.astype(ml_dtypes.float8_e4m3fn).view(np.uint8)
    else:
        c = by_word.astype(ml_dtypes.float4_e2m1fn).view(np.uint8) & 0xF
        words = (c[..., 0::2] | (c[..., 1::2] << 4)).reshape(k // 512, 128, 2 * n)
    return np.ascontiguousarray(words), np.ascontiguousarray(byte.astype(np.uint8).reshape(k // 512, 16, n))


def unpack_weight(words, scales, fmt):
    g, _, n = scales.shape
    words = np.ascontiguousarray(words).reshape(g, 128, n, -1)
    if fmt == "e4m3":
        vals = words.view(ml_dtypes.float8_e4m3fn).astype(np.float64)
    else:
        nib = np.empty((g, 128, n, 4), np.uint8)
        nib[..., 0::2] = words & 0xF
        nib[..., 1::2] = words >> 4
        vals = E2M1[nib]
    vals = vals * np.repeat(np.exp2(scales.astype(np.float64) - 127.0), 8, axis=1)[..., None]
    return vals.transpose(0, 1, 3, 2).reshape(g * 512, n)


D, T, I, Q, G = 512, 1024, 512, 128, 64


def setup_inputs():
    n = np.random.standard_normal
    idx = np.stack([np.random.permutation(T)[:I] for _ in range(8)])
    idx2 = np.stack([np.random.permutation(T)[:I] for _ in range(8)])
    idx3 = np.stack([np.random.permutation(T)[:I] for _ in range(8)])
    idx4 = np.stack([np.random.permutation(T)[:I] for _ in range(8)])
    fd = mx_kscale(D)
    keysp = pack_weight(n((D, T)) / fd[:, None], "e2m1")
    return {
        "query": (n((D, Q)) * 1.0 / np.sqrt(D) * fd[:, None]).astype(np.float32),
        "keys_words": keysp[0],
        "keys_scales": keysp[1],
        "lam": (np.random.uniform(0.3, 0.9, (Q, 1))).astype(np.float32),
        "old": (np.random.uniform(0.0, 2.0, (Q, T))).astype(np.float32),
        "gainm": (np.random.uniform(0.5, 1.5, (Q, I))).astype(np.float32),
        "offs": striped8(idx),
        "offs2": striped8(idx2),
        "offs3": striped8(idx3),
        "offs4": striped8(idx4),
    }


def reference(query, keys_words, keys_scales, lam, old, gainm, offs, offs2, offs3, offs4):
    idx = unstriped8(offs)
    idx2 = unstriped8(offs2)
    idx3 = unstriped8(offs3)
    idx4 = unstriped8(offs4)
    keysu = unpack_weight(keys_words, keys_scales, "e2m1")
    queryq = mxq(f64(query), 0, "e4m3")
    a = queryq.T @ keysu
    rv = np.log(np.exp(pick8(a, idx2, 16)) + np.exp(pick8(a, idx3, 16)))
    s = pick8(a, idx, 16) - rv * f64(lam)
    p = np.exp(s)
    pg = p.reshape(Q, G, I // G).sum(axis=2)
    rt0 = np.sqrt(pg)
    k0 = rt0 / np.sum(rt0, axis=1, keepdims=True) / np.square(pg)
    kr = np.repeat(k0, I // G, axis=1)
    w = np.square(p) * kr
    ws = w * f64(gainm) * 128.0
    wf = np.zeros((Q, T))
    wf[np.arange(Q)[:, None], idx4[np.arange(Q) % 128 // 16]] = ws
    y = f64(old) + wf
    return y

@@ -1,0 +1,139 @@
+from contextlib import ExitStack
+
+import concourse.mybir as mybir
+
+D, T, I, Q, G = 512, 1024, 512, 128, 64
+RUN = I // G
+P = 128
+PACK = 4
+N_TILE = 256
+FLOPS = 2 * D * T * Q
+
+F32 = mybir.dt.float32
+BF16 = mybir.dt.bfloat16
+I32 = mybir.dt.int32
+U32 = mybir.dt.uint32
+U16 = mybir.dt.uint16
+U8 = mybir.dt.uint8
+FP8X4 = mybir.dt.float8_e4m3fn_x4
+FP4X4 = mybir.dt.float4_e2m1fn_x4
+ACT = mybir.ActivationFunctionType
+ALU = mybir.AluOpType
+AX = mybir.AxisListType
+
+
+def tile_attend_tworivals_pagewinners_moved_heads_kernel(
+    tc, query, keys_words, keys_scales, lam, old, gainm, offs, offs2, offs3, offs4, out
+):
+    nc = tc.nc
+    with ExitStack() as ctx:
+        sb = ctx.enter_context(tc.tile_pool(name="sb", bufs=1))
+        ps = ctx.enter_context(tc.psum_pool(name="ps", bufs=1))
+
+        q_raw = sb.tile([P, PACK, Q], F32, name="q_raw")
+        nc.sync.dma_start(out=q_raw[:], in_=query.rearrange("(p j) q -> p j q", j=PACK))
+        k_words = sb.tile([P, 2 * T], U8, name="k_words", align_bytes=64)
+        nc.sync.dma_start(out=k_words[:].bitcast(I32), in_=keys_words[0].bitcast(I32))
+        k_scales = sb.tile([P, T], U8, name="k_scales", align_bytes=64)
+        nc.vector.memset(k_scales[:].bitcast(I32), 0)
+        for quad in range(4):
+            nc.scalar.dma_start(
+                out=k_scales[32 * quad : 32 * quad + 4, :].bitcast(I32),
+                in_=keys_scales[0, 4 * quad : 4 * quad + 4, :].bitcast(I32),
+            )
+        list2 = sb.tile([P, I // 16], U16, name="list2")
+        nc.sync.dma_start(list2[:], offs2)
+        list3 = sb.tile([P, I // 16], U16, name="list3")
+        nc.sync.dma_start(list3[:], offs3)
+        list1 = sb.tile([P, I // 16], U16, name="list1")
+        nc.sync.dma_start(list1[:], offs)
+        lam_t = sb.tile([P, 1], F32, name="lam_t")
+        nc.sync.dma_start(out=lam_t[:], in_=lam)
+        gain = sb.tile([P, I], F32, name="gain")
+        nc.sync.dma_start(out=gain[:], in_=gainm)
+        list4 = sb.tile([P, I // 16], U16, name="list4")
+        nc.sync.dma_start(list4[:], offs4)
+        old_t = sb.tile([P, T], F32, name="old_t")
+        nc.sync.dma_start(out=old_t[:], in_=old)
+
+        wf = sb.tile([P, T], F32, name="wf")
+        nc.vector.memset(wf[:], 0.0)
+
+        q_bf = sb.tile([P, Q, PACK], BF16, name="q_bf", align_bytes=64)
+        nc.vector.tensor_copy(out=q_bf[:], in_=q_raw[:].rearrange("p j q -> p q j"))
+        q_codes = sb.tile([P, Q], U32, name="q_codes", align_bytes=64)
+        q_scales = sb.tile([P, Q], U8, name="q_scales", align_bytes=64)
+        nc.vector.quantize_mx(
+            out=q_codes[:].bitcast(FP8X4),
+            scales=q_scales[:],
+            in_=q_bf[:].rearrange("p q j -> p (q j)"),
+        )
+
+        a = sb.tile([P, T], F32, name="a")
+        for b in range(T // N_TILE):
+            cols = slice(b * N_TILE, (b + 1) * N_TILE)
+            bank = ps.tile([P, N_TILE], F32, name=f"bank{b}")
+            nc.tensor.matmul_mx(
+                out=bank[:],
+                lhsT=q_codes[:].bitcast(FP8X4),
+                lhsT_scale=q_scales[:],
+                rhs=k_words[:, 2 * b * N_TILE : 2 * (b + 1) * N_TILE].bitcast(FP4X4),
+                rhs_scale=k_scales[:, cols],
+                start=True,
+                stop=True,
+            )
+            if b % 2 == 0:
+                nc.vector.tensor_copy(out=a[:, cols], in_=bank[:])
+            else:
+                nc.scalar.copy(out=a[:, cols], in_=bank[:])
+
+        neg_lam = sb.tile([P, 1], F32, name="neg_lam")
+        nc.vector.tensor_scalar(out=neg_lam[:], in0=lam_t[:], scalar1=-1.0, scalar2=None, op0=ALU.mult)
+
+        e2 = sb.tile([P, I], F32, name="e2")
+        nc.scalar.activation(e2[:], a[:].indirect(list2[:]), ACT.Exp)
+        a3 = sb.tile([P, I], F32, name="a3")
+        nc.vector.tensor_copy(a3[:], a[:].indirect(list3[:]))
+        e3 = sb.tile([P, I], F32, name="e3")
+        nc.scalar.activation(e3[:], a3[:], ACT.Exp)
+        a1 = sb.tile([P, I], F32, name="a1")
+        nc.vector.tensor_copy(a1[:], a[:].indirect(list1[:]))
+        x = sb.tile([P, I], F32, name="x")
+        nc.vector.tensor_tensor(x[:], e2[:], e3[:], ALU.add)
+        rv = sb.tile([P, I], F32, name="rv")
+        nc.scalar.activation(rv[:], x[:], ACT.Ln)
+        s = sb.tile([P, I], F32, name="s")
+        nc.vector.scalar_tensor_tensor(s[:], rv[:], neg_lam[:], a1[:], ALU.mult, ALU.add)
+        p = sb.tile([P, G, RUN], F32, name="p")
+        nc.scalar.activation(p[:].rearrange("p g r -> p (g r)"), s[:], ACT.Exp)
+        p2 = sb.tile([P, I], F32, name="p2")
+        nc.scalar.activation(p2[:], s[:], ACT.Exp, scale=2.0)
+        pg = sb.tile([P, G], F32, name="pg")
+        nc.vector.tensor_reduce(pg[:], p[:], AX.X, ALU.add)
+        rt = sb.tile([P, G], F32, name="rt")
+        rt_sum = sb.tile([P, 1], F32, name="rt_sum")
+        nc.scalar.activation(rt[:], pg[:], ACT.Sqrt, accum_out=rt_sum[:])
+        inv_pg = sb.tile([P, G], F32, name="inv_pg")
+        nc.vector.reciprocal(inv_pg[:], pg[:])
+        inv_pg2 = sb.tile([P, G], F32, name="inv_pg2")
+        nc.vector.scalar_tensor_tensor(inv_pg2[:], inv_pg[:], 128.0, inv_pg[:], ALU.mult, ALU.mult)
+        inv_sum = sb.tile([P, 1], F32, name="inv_sum")
+        nc.vector.reciprocal(inv_sum[:], rt_sum[:])
+        k0 = sb.tile([P, G], F32, name="k0")
+        nc.vector.scalar_tensor_tensor(k0[:], rt[:], inv_sum[:], inv_pg2[:], ALU.mult, ALU.mult)
+        gk = sb.tile([P, G, RUN], F32, name="gk")
+        nc.vector.tensor_tensor(
+            gk[:],
+            gain[:].rearrange("p (g r) -> p g r", r=RUN),
+            k0[:].unsqueeze(2).to_broadcast([P, G, RUN]),
+            ALU.mult,
+        )
+        nc.vector.tensor_tensor(
+            wf[:].indirect(list4[:]), p2[:], gk[:].rearrange("p g r -> p (g r)"), ALU.mult
+        )
+        for b in range(T // N_TILE):
+            cols = slice(b * N_TILE, (b + 1) * N_TILE)
+            res = sb.tile([P, N_TILE], F32, name=f"res{b}")
+            nc.vector.tensor_tensor(res[:], wf[:, cols], old_t[:, cols], ALU.add)
+            queue = nc.sync if b % 2 == 0 else nc.scalar
+            queue.dma_start(out=out[:, cols], in_=res[:])

@@ -7,6 +7,11 @@ RUN = I // G
 P = 128
 PACK = 4
 N_TILE = 256
+LIFT = 2.0**43
+FLOOR = 2.0**-86
+Q_SPLIT = 80
+PRODUCT_WIDTHS = (256, 256, 256, 128, 128)
+STORE_WIDTHS = (384, 256, 256, 128)
 FLOPS = 2 * D * T * Q
 
 F32 = mybir.dt.float32
@@ -22,6 +27,11 @@ ALU = mybir.AluOpType
 AX = mybir.AxisListType
 
 
+def column_runs(widths):
+    starts = [sum(widths[:n]) for n in range(len(widths))]
+    return [slice(s, s + w) for s, w in zip(starts, widths)]
+
+
 def tile_attend_tworivals_pagewinners_moved_heads_kernel(
     tc, query, keys_words, keys_scales, lam, old, gainm, offs, offs2, offs3, offs4, out
 ):
@@ -35,9 +45,9 @@ def tile_attend_tworivals_pagewinners_moved_heads_kernel(
         k_words = sb.tile([P, 2 * T], U8, name="k_words", align_bytes=64)
         nc.sync.dma_start(out=k_words[:].bitcast(I32), in_=keys_words[0].bitcast(I32))
         k_scales = sb.tile([P, T], U8, name="k_scales", align_bytes=64)
-        nc.vector.memset(k_scales[:].bitcast(I32), 0)
+        nc.gpsimd.memset(k_scales[:].bitcast(I32), 0)
         for quad in range(4):
-            nc.scalar.dma_start(
+            nc.sync.dma_start(
                 out=k_scales[32 * quad : 32 * quad + 4, :].bitcast(I32),
                 in_=keys_scales[0, 4 * quad : 4 * quad + 4, :].bitcast(I32),
             )
@@ -60,7 +70,8 @@ def tile_attend_tworivals_pagewinners_moved_heads_kernel(
         nc.vector.memset(wf[:], 0.0)
 
         q_bf = sb.tile([P, Q, PACK], BF16, name="q_bf", align_bytes=64)
-        nc.vector.tensor_copy(out=q_bf[:], in_=q_raw[:].rearrange("p j q -> p q j"))
+        nc.vector.tensor_copy(out=q_bf[:, :Q_SPLIT, :], in_=q_raw[:, :, :Q_SPLIT].rearrange("p j q -> p q j"))
+        nc.scalar.copy(out=q_bf[:, Q_SPLIT:, :], in_=q_raw[:, :, Q_SPLIT:].rearrange("p j q -> p q j"))
         q_codes = sb.tile([P, Q], U32, name="q_codes", align_bytes=64)
         q_scales = sb.tile([P, Q], U8, name="q_scales", align_bytes=64)
         nc.vector.quantize_mx(
@@ -70,14 +81,13 @@ def tile_attend_tworivals_pagewinners_moved_heads_kernel(
         )
 
         a = sb.tile([P, T], F32, name="a")
-        for b in range(T // N_TILE):
-            cols = slice(b * N_TILE, (b + 1) * N_TILE)
-            bank = ps.tile([P, N_TILE], F32, name=f"bank{b}")
+        for b, cols in enumerate(column_runs(PRODUCT_WIDTHS)):
+            bank = ps.tile([P, cols.stop - cols.start], F32, name=f"bank{b}")
             nc.tensor.matmul_mx(
                 out=bank[:],
                 lhsT=q_codes[:].bitcast(FP8X4),
                 lhsT_scale=q_scales[:],
-                rhs=k_words[:, 2 * b * N_TILE : 2 * (b + 1) * N_TILE].bitcast(FP4X4),
+                rhs=k_words[:, 2 * cols.start : 2 * cols.stop].bitcast(FP4X4),
                 rhs_scale=k_scales[:, cols],
                 start=True,
                 stop=True,
@@ -90,50 +100,77 @@ def tile_attend_tworivals_pagewinners_moved_heads_kernel(
         neg_lam = sb.tile([P, 1], F32, name="neg_lam")
         nc.vector.tensor_scalar(out=neg_lam[:], in0=lam_t[:], scalar1=-1.0, scalar2=None, op0=ALU.mult)
 
+        half = I // 2
+        halves = [slice(0, half), slice(half, I)]
         e2 = sb.tile([P, I], F32, name="e2")
         nc.scalar.activation(e2[:], a[:].indirect(list2[:]), ACT.Exp)
         a3 = sb.tile([P, I], F32, name="a3")
-        nc.vector.tensor_copy(a3[:], a[:].indirect(list3[:]))
         e3 = sb.tile([P, I], F32, name="e3")
-        nc.scalar.activation(e3[:], a3[:], ACT.Exp)
+        for h in halves:
+            nc.vector.tensor_copy(a3[:, h], a[:].indirect(list3[:, h.start // 16 : h.stop // 16]))
+            nc.scalar.activation(e3[:, h], a3[:, h], ACT.Exp)
         a1 = sb.tile([P, I], F32, name="a1")
         nc.vector.tensor_copy(a1[:], a[:].indirect(list1[:]))
         x = sb.tile([P, I], F32, name="x")
-        nc.vector.tensor_tensor(x[:], e2[:], e3[:], ALU.add)
         rv = sb.tile([P, I], F32, name="rv")
-        nc.scalar.activation(rv[:], x[:], ACT.Ln)
         s = sb.tile([P, I], F32, name="s")
-        nc.vector.scalar_tensor_tensor(s[:], rv[:], neg_lam[:], a1[:], ALU.mult, ALU.add)
-        p = sb.tile([P, G, RUN], F32, name="p")
-        nc.scalar.activation(p[:].rearrange("p g r -> p (g r)"), s[:], ACT.Exp)
-        p2 = sb.tile([P, I], F32, name="p2")
-        nc.scalar.activation(p2[:], s[:], ACT.Exp, scale=2.0)
+        for h in halves:
+            nc.vector.tensor_tensor(x[:, h], e2[:, h], e3[:, h], ALU.add)
+        for h in halves:
+            nc.scalar.activation(rv[:, h], x[:, h], ACT.Ln)
+        for h in halves:
+            nc.vector.scalar_tensor_tensor(s[:, h], rv[:, h], neg_lam[:], a1[:, h], ALU.mult, ALU.add)
+        neg_max = sb.tile([P, 1], F32, name="neg_max")
+        nc.vector.tensor_reduce(neg_max[:], s[:], AX.X, ALU.max, negate=True)
+        p = sb.tile([P, I], F32, name="p")
         pg = sb.tile([P, G], F32, name="pg")
-        nc.vector.tensor_reduce(pg[:], p[:], AX.X, ALU.add)
+        pgain = sb.tile([P, I], F32, name="pgain")
+        p2gain = sb.tile([P, I], F32, name="p2gain")
+        for h in halves:
+            nc.scalar.activation(p[:, h], s[:, h], ACT.Exp, bias=neg_max[:])
+        for h in halves:
+            nc.vector.tensor_reduce(
+                pg[:, h.start // RUN : h.stop // RUN],
+                p[:, h].rearrange("p (g r) -> p g r", r=RUN),
+                AX.X,
+                ALU.add,
+            )
+        pg2 = sb.tile([P, G], F32, name="pg2")
+        nc.vector.scalar_tensor_tensor(pg2[:], pg[:], LIFT, pg[:], ALU.mult, ALU.mult)
+        pg3 = sb.tile([P, G], F32, name="pg3")
+        nc.vector.scalar_tensor_tensor(pg3[:], pg2[:], LIFT, pg[:], ALU.mult, ALU.mult)
+        for h in halves:
+            nc.vector.tensor_tensor(pgain[:, h], p[:, h], gain[:, h], ALU.mult)
+        for h in halves:
+            nc.vector.tensor_tensor(p2gain[:, h], pgain[:, h], p[:, h], ALU.mult)
+        kr = sb.tile([P, G, RUN], F32, name="kr")
+        kr_flat = kr[:].rearrange("p g r -> p (g r)")
+        pieces = [slice(0, 128), slice(128, I)]
+        for c in pieces:
+            runs = slice(c.start // RUN, c.stop // RUN)
+            nc.scalar.activation(
+                kr[:, runs, :],
+                pg3[:, runs].unsqueeze(2).to_broadcast([P, runs.stop - runs.start, RUN]),
+                ACT.Abs_reciprocal_sqrt,
+                bias=FLOOR,
+            )
+        c = pieces[0]
+        nc.vector.tensor_tensor(
+            wf[:].indirect(list4[:, c.start // 16 : c.stop // 16]), p2gain[:, c], kr_flat[:, c], ALU.mult
+        )
         rt = sb.tile([P, G], F32, name="rt")
         rt_sum = sb.tile([P, 1], F32, name="rt_sum")
-        nc.scalar.activation(rt[:], pg[:], ACT.Sqrt, accum_out=rt_sum[:])
-        inv_pg = sb.tile([P, G], F32, name="inv_pg")
-        nc.vector.reciprocal(inv_pg[:], pg[:])
-        inv_pg2 = sb.tile([P, G], F32, name="inv_pg2")
-        nc.vector.scalar_tensor_tensor(inv_pg2[:], inv_pg[:], 128.0, inv_pg[:], ALU.mult, ALU.mult)
-        inv_sum = sb.tile([P, 1], F32, name="inv_sum")
-        nc.vector.reciprocal(inv_sum[:], rt_sum[:])
-        k0 = sb.tile([P, G], F32, name="k0")
-        nc.vector.scalar_tensor_tensor(k0[:], rt[:], inv_sum[:], inv_pg2[:], ALU.mult, ALU.mult)
-        gk = sb.tile([P, G, RUN], F32, name="gk")
-        nc.vector.tensor_tensor(
-            gk[:],
-            gain[:].rearrange("p (g r) -> p g r", r=RUN),
-            k0[:].unsqueeze(2).to_broadcast([P, G, RUN]),
-            ALU.mult,
+        nc.vector.scalar_tensor_tensor(
+            rt[:], pg2[:], 1.0 / (128.0 * LIFT), kr[:, :, 0], ALU.mult, ALU.mult, accum_out=rt_sum[:]
         )
+        c = pieces[1]
         nc.vector.tensor_tensor(
-            wf[:].indirect(list4[:]), p2[:], gk[:].rearrange("p g r -> p (g r)"), ALU.mult
+            wf[:].indirect(list4[:, c.start // 16 : c.stop // 16]), p2gain[:, c], kr_flat[:, c], ALU.mult
         )
-        for b in range(T // N_TILE):
-            cols = slice(b * N_TILE, (b + 1) * N_TILE)
-            res = sb.tile([P, N_TILE], F32, name=f"res{b}")
-            nc.vector.tensor_tensor(res[:], wf[:, cols], old_t[:, cols], ALU.add)
+        norm = sb.tile([P, 1], F32, name="norm")
+        nc.vector.reciprocal(norm[:], rt_sum[:])
+        for b, cols in enumerate(column_runs(STORE_WIDTHS)):
+            res = sb.tile([P, cols.stop - cols.start], F32, name=f"res{b}")
+            nc.vector.scalar_tensor_tensor(res[:], wf[:, cols], norm[:], old_t[:, cols], ALU.mult, ALU.add)
             queue = nc.sync if b % 2 == 0 else nc.scalar
             queue.dma_start(out=out[:, cols], in_=res[:])

@@ -43,14 +43,15 @@ def tile_attend_tworivals_pagewinners_moved_heads_kernel(
         q_raw = sb.tile([P, PACK, Q], F32, name="q_raw")
         nc.sync.dma_start(out=q_raw[:], in_=query.rearrange("(p j) q -> p j q", j=PACK))
         k_words = sb.tile([P, 2 * T], U8, name="k_words", align_bytes=64)
-        nc.sync.dma_start(out=k_words[:].bitcast(I32), in_=keys_words[0].bitcast(I32))
+        nc.sync.dma_start(out=k_words[:, :T].bitcast(I32), in_=keys_words[0, :, :T].bitcast(I32))
         k_scales = sb.tile([P, T], U8, name="k_scales", align_bytes=64)
-        nc.gpsimd.memset(k_scales[:].bitcast(I32), 0)
+        nc.vector.memset(k_scales[:].bitcast(I32), 0)
         for quad in range(4):
             nc.sync.dma_start(
                 out=k_scales[32 * quad : 32 * quad + 4, :].bitcast(I32),
                 in_=keys_scales[0, 4 * quad : 4 * quad + 4, :].bitcast(I32),
             )
+        nc.sync.dma_start(out=k_words[:, T:].bitcast(I32), in_=keys_words[0, :, T:].bitcast(I32))
         list2 = sb.tile([P, I // 16], U16, name="list2")
         nc.sync.dma_start(list2[:], offs2)
         list3 = sb.tile([P, I // 16], U16, name="list3")

@@ -11,7 +11,7 @@ LIFT = 2.0**43
 FLOOR = 2.0**-86
 Q_SPLIT = 80
 PRODUCT_WIDTHS = (256, 256, 256, 128, 128)
-STORE_WIDTHS = (384, 256, 256, 128)
+STORE_WIDTHS = (128, 256, 320, 320)
 FLOPS = 2 * D * T * Q
 
 F32 = mybir.dt.float32

from contextlib import ExitStack

import concourse.mybir as mybir

D, T, I, Q, G = 512, 1024, 512, 128, 64
RUN = I // G
P = 128
PACK = 4
N_TILE = 256
LIFT = 2.0**43
FLOOR = 2.0**-86
Q_SPLIT = 80
PRODUCT_WIDTHS = (256, 256, 256, 128, 128)
STORE_WIDTHS = (128, 256, 320, 320)
FLOPS = 2 * D * T * Q

F32 = mybir.dt.float32
BF16 = mybir.dt.bfloat16
I32 = mybir.dt.int32
U32 = mybir.dt.uint32
U16 = mybir.dt.uint16
U8 = mybir.dt.uint8
FP8X4 = mybir.dt.float8_e4m3fn_x4
FP4X4 = mybir.dt.float4_e2m1fn_x4
ACT = mybir.ActivationFunctionType
ALU = mybir.AluOpType
AX = mybir.AxisListType


def column_runs(widths):
    starts = [sum(widths[:n]) for n in range(len(widths))]
    return [slice(s, s + w) for s, w in zip(starts, widths)]


def tile_attend_tworivals_pagewinners_moved_heads_kernel(
    tc, query, keys_words, keys_scales, lam, old, gainm, offs, offs2, offs3, offs4, out
):
    nc = tc.nc
    with ExitStack() as ctx:
        sb = ctx.enter_context(tc.tile_pool(name="sb", bufs=1))
        ps = ctx.enter_context(tc.psum_pool(name="ps", bufs=1))

        q_raw = sb.tile([P, PACK, Q], F32, name="q_raw")
        nc.sync.dma_start(out=q_raw[:], in_=query.rearrange("(p j) q -> p j q", j=PACK))
        k_words = sb.tile([P, 2 * T], U8, name="k_words", align_bytes=64)
        nc.sync.dma_start(out=k_words[:, :T].bitcast(I32), in_=keys_words[0, :, :T].bitcast(I32))
        k_scales = sb.tile([P, T], U8, name="k_scales", align_bytes=64)
        nc.vector.memset(k_scales[:].bitcast(I32), 0)
        for quad in range(4):
            nc.sync.dma_start(
                out=k_scales[32 * quad : 32 * quad + 4, :].bitcast(I32),
                in_=keys_scales[0, 4 * quad : 4 * quad + 4, :].bitcast(I32),
            )
        nc.sync.dma_start(out=k_words[:, T:].bitcast(I32), in_=keys_words[0, :, T:].bitcast(I32))
        list2 = sb.tile([P, I // 16], U16, name="list2")
        nc.sync.dma_start(list2[:], offs2)
        list3 = sb.tile([P, I // 16], U16, name="list3")
        nc.sync.dma_start(list3[:], offs3)
        list1 = sb.tile([P, I // 16], U16, name="list1")
        nc.sync.dma_start(list1[:], offs)
        lam_t = sb.tile([P, 1], F32, name="lam_t")
        nc.sync.dma_start(out=lam_t[:], in_=lam)
        gain = sb.tile([P, I], F32, name="gain")
        nc.sync.dma_start(out=gain[:], in_=gainm)
        list4 = sb.tile([P, I // 16], U16, name="list4")
        nc.sync.dma_start(list4[:], offs4)
        old_t = sb.tile([P, T], F32, name="old_t")
        nc.sync.dma_start(out=old_t[:], in_=old)

        wf = sb.tile([P, T], F32, name="wf")
        nc.vector.memset(wf[:], 0.0)

        q_bf = sb.tile([P, Q, PACK], BF16, name="q_bf", align_bytes=64)
        nc.vector.tensor_copy(out=q_bf[:, :Q_SPLIT, :], in_=q_raw[:, :, :Q_SPLIT].rearrange("p j q -> p q j"))
        nc.scalar.copy(out=q_bf[:, Q_SPLIT:, :], in_=q_raw[:, :, Q_SPLIT:].rearrange("p j q -> p q j"))
        q_codes = sb.tile([P, Q], U32, name="q_codes", align_bytes=64)
        q_scales = sb.tile([P, Q], U8, name="q_scales", align_bytes=64)
        nc.vector.quantize_mx(
            out=q_codes[:].bitcast(FP8X4),
            scales=q_scales[:],
            in_=q_bf[:].rearrange("p q j -> p (q j)"),
        )

        a = sb.tile([P, T], F32, name="a")
        for b, cols in enumerate(column_runs(PRODUCT_WIDTHS)):
            bank = ps.tile([P, cols.stop - cols.start], F32, name=f"bank{b}")
            nc.tensor.matmul_mx(
                out=bank[:],
                lhsT=q_codes[:].bitcast(FP8X4),
                lhsT_scale=q_scales[:],
                rhs=k_words[:, 2 * cols.start : 2 * cols.stop].bitcast(FP4X4),
                rhs_scale=k_scales[:, cols],
                start=True,
                stop=True,
            )
            if b % 2 == 0:
                nc.vector.tensor_copy(out=a[:, cols], in_=bank[:])
            else:
                nc.scalar.copy(out=a[:, cols], in_=bank[:])

        neg_lam = sb.tile([P, 1], F32, name="neg_lam")
        nc.vector.tensor_scalar(out=neg_lam[:], in0=lam_t[:], scalar1=-1.0, scalar2=None, op0=ALU.mult)

        half = I // 2
        halves = [slice(0, half), slice(half, I)]
        e2 = sb.tile([P, I], F32, name="e2")
        nc.scalar.activation(e2[:], a[:].indirect(list2[:]), ACT.Exp)
        a3 = sb.tile([P, I], F32, name="a3")
        e3 = sb.tile([P, I], F32, name="e3")
        for h in halves:
            nc.vector.tensor_copy(a3[:, h], a[:].indirect(list3[:, h.start // 16 : h.stop // 16]))
            nc.scalar.activation(e3[:, h], a3[:, h], ACT.Exp)
        a1 = sb.tile([P, I], F32, name="a1")
        nc.vector.tensor_copy(a1[:], a[:].indirect(list1[:]))
        x = sb.tile([P, I], F32, name="x")
        rv = sb.tile([P, I], F32, name="rv")
        s = sb.tile([P, I], F32, name="s")
        for h in halves:
            nc.vector.tensor_tensor(x[:, h], e2[:, h], e3[:, h], ALU.add)
        for h in halves:
            nc.scalar.activation(rv[:, h], x[:, h], ACT.Ln)
        for h in halves:
            nc.vector.scalar_tensor_tensor(s[:, h], rv[:, h], neg_lam[:], a1[:, h], ALU.mult, ALU.add)
        neg_max = sb.tile([P, 1], F32, name="neg_max")
        nc.vector.tensor_reduce(neg_max[:], s[:], AX.X, ALU.max, negate=True)
        p = sb.tile([P, I], F32, name="p")
        pg = sb.tile([P, G], F32, name="pg")
        pgain = sb.tile([P, I], F32, name="pgain")
        p2gain = sb.tile([P, I], F32, name="p2gain")
        for h in halves:
            nc.scalar.activation(p[:, h], s[:, h], ACT.Exp, bias=neg_max[:])
        for h in halves:
            nc.vector.tensor_reduce(
                pg[:, h.start // RUN : h.stop // RUN],
                p[:, h].rearrange("p (g r) -> p g r", r=RUN),
                AX.X,
                ALU.add,
            )
        pg2 = sb.tile([P, G], F32, name="pg2")
        nc.vector.scalar_tensor_tensor(pg2[:], pg[:], LIFT, pg[:], ALU.mult, ALU.mult)
        pg3 = sb.tile([P, G], F32, name="pg3")
        nc.vector.scalar_tensor_tensor(pg3[:], pg2[:], LIFT, pg[:], ALU.mult, ALU.mult)
        for h in halves:
            nc.vector.tensor_tensor(pgain[:, h], p[:, h], gain[:, h], ALU.mult)
        for h in halves:
            nc.vector.tensor_tensor(p2gain[:, h], pgain[:, h], p[:, h], ALU.mult)
        kr = sb.tile([P, G, RUN], F32, name="kr")
        kr_flat = kr[:].rearrange("p g r -> p (g r)")
        pieces = [slice(0, 128), slice(128, I)]
        for c in pieces:
            runs = slice(c.start // RUN, c.stop // RUN)
            nc.scalar.activation(
                kr[:, runs, :],
                pg3[:, runs].unsqueeze(2).to_broadcast([P, runs.stop - runs.start, RUN]),
                ACT.Abs_reciprocal_sqrt,
                bias=FLOOR,
            )
        c = pieces[0]
        nc.vector.tensor_tensor(
            wf[:].indirect(list4[:, c.start // 16 : c.stop // 16]), p2gain[:, c], kr_flat[:, c], ALU.mult
        )
        rt = sb.tile([P, G], F32, name="rt")
        rt_sum = sb.tile([P, 1], F32, name="rt_sum")
        nc.vector.scalar_tensor_tensor(
            rt[:], pg2[:], 1.0 / (128.0 * LIFT), kr[:, :, 0], ALU.mult, ALU.mult, accum_out=rt_sum[:]
        )
        c = pieces[1]
        nc.vector.tensor_tensor(
            wf[:].indirect(list4[:, c.start // 16 : c.stop // 16]), p2gain[:, c], kr_flat[:, c], ALU.mult
        )
        norm = sb.tile([P, 1], F32, name="norm")
        nc.vector.reciprocal(norm[:], rt_sum[:])
        for b, cols in enumerate(column_runs(STORE_WIDTHS)):
            res = sb.tile([P, cols.stop - cols.start], F32, name=f"res{b}")
            nc.vector.scalar_tensor_tensor(res[:], wf[:, cols], norm[:], old_t[:, cols], ALU.mult, ALU.add)
            queue = nc.sync if b % 2 == 0 else nc.scalar
            queue.dma_start(out=out[:, cols], in_=res[:])
